import numpy as np
import ml_dtypes


def mxq(x, axis, fmt="e4m3"):
    dtype, down = {"e4m3": (ml_dtypes.float8_e4m3fn, 7), "e5m2": (ml_dtypes.float8_e5m2, 14)}[fmt]
    v = np.moveaxis(np.asarray(x, np.float32).astype(ml_dtypes.bfloat16).astype(np.float64), axis, -1)
    blocks = v.reshape(v.shape[:-1] + (-1, 32))
    amax = np.abs(blocks).max(-1, keepdims=True)
    byte = np.maximum(np.where(amax > 0, np.frexp(amax)[1] - 1 + 127, 0) - down, 1)
    scale = np.exp2(byte - 127.0)
    codes = (blocks / scale).astype(np.float32).astype(dtype).astype(np.float64)
    return np.moveaxis((codes * scale).reshape(v.shape), -1, axis)


WIDE = False


def mx_kscale(k):
    if not WIDE:
        return np.ones(k)
    levels = np.array([10, -10, 5, -5, 0])
    if k % 512:
        return np.exp2(np.random.permutation(np.resize(levels, k // 32))).repeat(32)
    a = np.empty((k // 512, 16))
    for p in range(k // 512):
        a[p, :8] = np.random.permutation(np.resize(levels, 8))
        for g in range(8):
            far = levels[np.abs(levels - a[p, g]) >= 10]
            a[p, g + 8] = far[np.random.randint(len(far))]
    return np.exp2(a.ravel()).repeat(32)


def f64(x):
    return np.asarray(x).astype(np.float64)


def striped(idx):
    return np.tile(idx.reshape(-1, 16).T, (8, 1)).astype(np.uint16)


def unstriped(offs):
    return offs[:16].T.reshape(-1).astype(np.int64)


def striped8(idx):
    return np.concatenate([x.reshape(-1, 16).T for x in idx]).astype(np.uint16)


def runs(offs, k):
    lists = np.stack([offs[16 * r : 16 * r + 16].T.reshape(-1) for r in range(8)]).astype(np.int64)
    return lists[np.arange(k) % 512 // 64]


def pack_weight(w):
    k, n = w.shape
    w = f64(np.asarray(w, np.float32).astype(ml_dtypes.bfloat16)).reshape(k // 32, 32, n)
    amax = np.abs(w).max(1)
    byte = np.clip(np.where(amax > 0, np.frexp(amax)[1] - 1 + 127 - 7, 1), 1, 254)
    scaled = (w * np.exp2(127.0 - byte)[:, None, :]).reshape(k, n).astype(np.float32)
    words = np.ascontiguousarray(scaled.reshape(k // 512, 128, 4, n).transpose(0, 1, 3, 2)).astype(ml_dtypes.float8_e4m3fn).view(np.uint8)
    return words, np.ascontiguousarray(byte.astype(np.uint8).reshape(k // 512, 16, n))


def unpack_weight(words, scales):
    g, p, n, _ = words.shape
    vals = np.ascontiguousarray(words).view(ml_dtypes.float8_e4m3fn).astype(np.float64) * np.repeat(np.exp2(scales.astype(np.float64) - 127.0), 8, axis=1)[..., None]
    return vals.transpose(0, 1, 3, 2).reshape(g * 512, n)

def planes(y):
    n, m = y.shape
    v = y.astype(np.float32).astype(ml_dtypes.bfloat16).astype(np.float64).reshape(n // 32, 32, m)
    top = np.abs(v).max(1)
    byte = np.clip(np.where(top > 0, np.frexp(top)[1] - 1 + 127 - 7, 1), 1, 254)
    codes = (v * np.exp2(127.0 - byte)[:, None, :]).reshape(n, m).astype(np.float32).astype(ml_dtypes.float8_e4m3fn).view(np.uint8)
    words = codes.reshape(n // 512, 128, 4, m).transpose(0, 1, 3, 2)
    return np.ascontiguousarray(words), np.ascontiguousarray(byte.astype(np.uint8).reshape(n // 512, 16, m))


K, T, S, N, H, W, G = 512, 2048, 256, 512, 512, 128, 1024


def setup_inputs():
    n = np.random.standard_normal
    s = mx_kscale(K)[:, None]
    u = mx_kscale(H)
    packed_xT = pack_weight(n((K, T)) * s)
    packed_w1 = pack_weight(n((K, H)) / np.sqrt(K) / s)
    packed_w2 = pack_weight(n((H, N)) / np.sqrt(2 * H) / u[:, None])
    packed_w3 = pack_weight(n((K, N)) / np.sqrt(2 * K) / s)
    perm = np.random.permutation(S)
    return {
        "x_words": packed_xT[0],
        "x_scales": packed_xT[1],
        "w1_words": packed_w1[0],
        "w1_scales": packed_w1[1],
        "gn": (np.random.uniform(0.5, 1.5, (H, 1)) * u[:, None]).astype(np.float32),
        "w2_words": packed_w2[0],
        "w2_scales": packed_w2[1],
        "w3_words": packed_w3[0],
        "w3_scales": packed_w3[1],
        "offs": striped(np.random.permutation(T)[:S]),
        "n1": striped(perm[:W]),
        "n2": striped(perm[W:]),
        "hz": striped8(np.random.randint(0, T, (8, S))),
        "n3": striped(np.random.randint(0, S, G)),
    }


def reference(x_words, x_scales, w1_words, w1_scales, gn, w2_words, w2_scales, w3_words, w3_scales, offs, n1, n2, hz, n3):
    xq = unpack_weight(x_words, x_scales)[:, unstriped(offs)]
    y = unpack_weight(w1_words, w1_scales).T @ xq
    pa = y[:, unstriped(n1)]
    pb = y[:, unstriped(n2)]
    rb = np.minimum(pa, pb)
    ra = np.maximum(pa, pb)
    ds = np.zeros((H, S))
    ds[:, unstriped(n1)] = ra
    dt = ds.copy()
    dt[:, unstriped(n2)] = rb
    z = f64(gn) * dt
    x_hz = unpack_weight(x_words, x_scales)[np.arange(K)[:, None], runs(hz, K)]
    h = unpack_weight(w2_words, w2_scales).T @ mxq(z, 0, "e4m3") + unpack_weight(w3_words, w3_scales).T @ x_hz
    ex = np.exp(0.5 * h)
    mb = ex[:, unstriped(n3)]
    ms = mb.reshape(N, S, 4).sum(axis=2)
    out_0 = (4.0 * ex) / (ms + 0.5)
    return (out_0,) + planes(out_0)

from contextlib import ExitStack

import concourse.mybir as mybir

K, T, S, N, H, W, G = 512, 2048, 256, 512, 512, 128, 1024
FLOPS = 2 * S * (K * H + H * N + K * N)

F32 = mybir.dt.float32
BF16 = mybir.dt.bfloat16
I32 = mybir.dt.int32
U32 = mybir.dt.uint32
U16 = mybir.dt.uint16
U8 = mybir.dt.uint8
FP8X4 = mybir.dt.float8_e4m3fn_x4
ALU = mybir.AluOpType
ACT = mybir.ActivationFunctionType

P = 128
PACK = 4
QUAD = 32
MEMBERS = 4
BLOCKS = ((0, 64), (64, 192), (192, 256))
WINDOW = 520
DOWN = 2.0**-124


def words_of(dram):
    return dram[0].rearrange("p c r -> p (c r)").bitcast(I32)


def load_scale_rows(queues, tile, first, dram):
    rows = dram[0].bitcast(I32)
    for q in range(4):
        queues[q].dma_start(
            out=tile[QUAD * q + first : QUAD * q + first + 4, :].bitcast(I32), in_=rows[4 * q : 4 * q + 4, :]
        )


def deal(nc, out, in_):
    nc.vector.tensor_copy(
        out=out.rearrange("p (t m) -> p m t", t=PACK), in_=in_.rearrange("p (m t) -> p m t", t=PACK)
    )


def tile_picked_mixhordergshare_none_po_kernel(
    tc, x_words, x_scales, w1_words, w1_scales, gn, w2_words, w2_scales, w3_words, w3_scales,
    offs, n1, n2, hz, n3, out_0, out_1, out_2,
):
    nc = tc.nc
    with ExitStack() as ctx:
        sb = ctx.enter_context(tc.tile_pool(name="sb", bufs=1))
        ps = ctx.enter_context(tc.psum_pool(name="ps", bufs=1))

        def tile(name, shape, dtype, tag=None):
            return sb.tile(shape, dtype, name=name, tag=tag or name, align_bytes=64)

        offs_t = tile("offs_t", [P, S // 16], U16)
        n1_t = tile("n1_t", [P, W // 16], U16)
        n2_t = tile("n2_t", [P, W // 16], U16)
        hz_t = tile("hz_t", [P, S // 16], U16)
        n3_t = tile("n3_t", [P, G // 16], U16)
        xw = tile("xw", [P, T], U32)
        xs = tile("xs", [P, T], U8, "xs_w2_z")
        xs_runs = tile("xs_runs", [P, T], U8)
        w1w_raw = tile("w1w_raw", [P, H], I32, "w1_w3")
        ws_raw = tile("ws_raw", [P, H], U8)
        hs = tile("hs", [P, S], U8)
        gain = tile("gain", [P, PACK], F32)
        ex = [tile("ex%d" % t, [P, WINDOW], F32) for t in range(PACK)]

        nc.vector.memset(xs[:].bitcast(I32), 0)
        nc.gpsimd.memset(ws_raw[:].bitcast(I32), 0)
        nc.vector.memset(ex[0][:, S:], 0.0)
        for t in range(1, PACK):
            nc.scalar.activation(ex[t][:, S:], ex[0][:, S:], ACT.Copy)
        nc.scalar.dma_start(out=xw[:].bitcast(I32), in_=words_of(x_words))
        nc.sync.dma_start(offs_t[:], offs)
        nc.sync.dma_start(out=w1w_raw[:], in_=words_of(w1_words))
        load_scale_rows([nc.sync] * 4, xs, 0, x_scales)
        load_scale_rows([nc.sync, nc.gpsimd, nc.gpsimd, nc.gpsimd], ws_raw, 0, w1_scales)
        nc.sync.dma_start(n1_t[:], n1)
        nc.sync.dma_start(n2_t[:], n2)
        nc.vector.memset(xs_runs[:].bitcast(I32), 0)
        nc.vector.memset(hs[:].bitcast(I32), 0)
        nc.sync.dma_start(hz_t[:], hz)
        nc.sync.dma_start(out=xs_runs[0:P:8, :].bitcast(I32), in_=x_scales[0].bitcast(I32))
        nc.gpsimd.dma_start(out=gain[:], in_=gn.rearrange("(p t) o -> p (t o)", t=PACK))
        nc.sync.dma_start(n3_t[:], n3)

        w1w = tile("w1w", [P, H], I32)
        w1s = tile("w1s", [P, H], U8)
        xqs = tile("xqs", [P, S], U8)
        xqw = tile("xqw", [P, S], U32)
        deal(nc, w1w[:], w1w_raw[:])
        nc.vector.tensor_copy(xqs[:], xs[:].indirect(offs_t[:]))
        deal(nc, w1s[:], ws_raw[:])
        nc.vector.tensor_copy(xqw[:], xw[:].indirect(offs_t[:]))

        w3w_raw = tile("w3w_raw", [P, N], I32, "w1_w3")
        w2w_raw = tile("w2w_raw", [P, N], I32, "xs_w2_z")
        load_scale_rows([nc.sync] * 4, ws_raw, 4, w2_scales)
        load_scale_rows([nc.sync] * 4, ws_raw, 8, w3_scales)
        nc.sync.dma_start(out=w3w_raw[:], in_=words_of(w3_words))
        nc.sync.dma_start(out=w2w_raw[:], in_=words_of(w2_words))

        y = []
        for t in range(PACK):
            cols = slice(P * t, P * (t + 1))
            y_ps = ps.tile([P, S], F32, name="y_ps%d" % t)
            nc.tensor.matmul_mx(
                out=y_ps[:], lhsT=w1w[:, cols].bitcast(FP8X4), lhsT_scale=w1s[:, cols],
                rhs=xqw[:].bitcast(FP8X4), rhs_scale=xqs[:], start=True, stop=True,
            )
            y.append(tile("y%d" % t, [P, S], F32))
            nc.vector.tensor_copy(out=y[t][:], in_=y_ps[:])

        ra, rb, dt = [], [], []

        def pair_up(t):
            pa = tile("pa%d" % t, [P, W], F32)
            pb = tile("pb%d" % t, [P, W], F32)
            nc.scalar.activation(pa[:], y[t][:].indirect(n1_t[:]), ACT.Copy)
            nc.scalar.activation(pb[:], y[t][:].indirect(n2_t[:]), ACT.Copy)
            ra.append(tile("ra%d" % t, [P, W], F32))
            rb.append(tile("rb%d" % t, [P, W], F32))
            nc.vector.tensor_tensor(ra[t][:], pa[:], pb[:], ALU.max)
            nc.vector.tensor_tensor(rb[t][:], pa[:], pb[:], ALU.min)

        def put_back(t):
            dt.append(tile("dt%d" % t, [P, S], F32))
            nc.scalar.activation(dt[t][:].indirect(n1_t[:]), ra[t][:], ACT.Copy)
            nc.scalar.activation(dt[t][:].indirect(n2_t[:]), rb[t][:], ACT.Copy)

        def round_z(t, cols=slice(0, S)):
            nc.vector.tensor_scalar(z[:, cols, t], dt[t][:, cols], gain[:, t : t + 1], None, ALU.mult)

        pair_up(0)
        pair_up(1)

        hw = tile("hw", [P, S], U32)
        hs_runs = tile("hs_runs", [P, S], U8)
        nc.vector.tensor_copy(hs_runs[:], xs_runs[:].indirect(hz_t[:]))
        nc.vector.tensor_copy(hw[:], xw[:].indirect(hz_t[:]))
        for r in range(4):
            nc.sync.dma_start(out=hs[r:P:QUAD, :].bitcast(I32), in_=hs_runs[8 * r : P : QUAD, :].bitcast(I32))

        put_back(0)
        pair_up(2)
        w2w = tile("w2w", [P, N], I32)
        w3w = tile("w3w", [P, N], I32)
        w23s = tile("w23s", [P, N], U8)
        deal(nc, w3w[:], w3w_raw[:])
        deal(nc, w23s[:], ws_raw[:])
        put_back(1)
        pair_up(3)
        deal(nc, w2w[:], w2w_raw[:])
        z = tile("z", [P, S, PACK], BF16, "xs_w2_z")
        round_z(0)
        round_z(1)
        h_ps = [ps.tile([P, S], F32, name="h_ps%d" % t) for t in range(PACK)]
        for t in range(PACK):
            cols = slice(P * t, P * (t + 1))
            nc.tensor.matmul_mx(
                out=h_ps[t][:], lhsT=w3w[:, cols].bitcast(FP8X4), lhsT_scale=w23s[8:P, cols],
                rhs=hw[:].bitcast(FP8X4), rhs_scale=hs[:], start=True, stop=False,
            )
        put_back(2)
        round_z(2)
        put_back(3)
        halves = (slice(0, S // 2), slice(S // 2, S))
        for cols in halves:
            round_z(3, cols)

        zw = tile("zw", [P, S], U32)
        zs = tile("zs", [P, S], U8)
        for cols in halves:
            nc.vector.quantize_mx(
                out=zw[:, cols].bitcast(FP8X4), scales=zs[:, cols], in_=z[:, cols, :].rearrange("p j t -> p (j t)")
            )
        for t in range(PACK):
            rows = slice(P * t, P * (t + 1))
            for cols in halves if t == 0 else (slice(0, S),):
                nc.tensor.matmul_mx(
                    out=h_ps[t][:, cols], lhsT=w2w[:, rows].bitcast(FP8X4), lhsT_scale=w23s[4:P, rows],
                    rhs=zw[:, cols].bitcast(FP8X4), rhs_scale=zs[:, cols], start=False, stop=cols.stop == S,
                )

        ow = tile("ow", [P, S], U32)
        osc = tile("osc", [P, S], U8)
        out_rows = out_0.rearrange("(p t) j -> p t j", t=PACK)
        out_words = words_of(out_1)
        res = [tile("res%d" % b, [P, PACK, c1 - c0], F32) for b, (c0, c1) in enumerate(BLOCKS)]

        units = [(b, a) for b in range(len(BLOCKS)) for a in range(2)]
        mb, part, den, prod, inv, fac = {}, {}, {}, {}, {}, {}

        def fetch(u):
            b, a = units[u]
            c0, c1 = BLOCKS[b]
            members = n3_t[:, MEMBERS * c0 // 16 : MEMBERS * c1 // 16]
            mb[u] = tile("mb%d" % u, [P, 2, c1 - c0, MEMBERS], F32)
            for i in range(2):
                t = 2 * a + i
                if b == 0:
                    nc.scalar.activation(ex[t][:, :S], h_ps[t][:], ACT.Exp, scale=0.5)
                nc.scalar.activation(mb[u][:, i].rearrange("p j m -> p (j m)"), ex[t][:].indirect(members), ACT.Copy)

        def add_pairs(u):
            width = mb[u].shape[2]
            part[u] = tile("part%d" % u, [P, 2 * width, 2], F32, "part")
            quads = mb[u][:].rearrange("p i j m -> p (i j) m")
            nc.vector.tensor_tensor(part[u][:], quads[:, :, 0:2], quads[:, :, 2:4], ALU.add)

        def denominators(u):
            width = mb[u].shape[2]
            den[u] = tile("den%d" % u, [P, 2, width], F32)
            nc.vector.scalar_tensor_tensor(
                den[u][:].rearrange("p i j -> p (i j)"), part[u][:, :, 0], 0.5, part[u][:, :, 1], ALU.add, ALU.add
            )

        def product(u):
            prod[u] = tile("prod%d" % u, [P, mb[u].shape[2]], F32)
            nc.vector.scalar_tensor_tensor(prod[u][:], den[u][:, 0], DOWN, den[u][:, 1], ALU.mult, ALU.mult)

        def invert(u):
            inv[u] = tile("inv%d" % u, [P, mb[u].shape[2]], F32)
            nc.vector.reciprocal(inv[u][:], prod[u][:])

        def factors(u):
            width = mb[u].shape[2]
            fac[u] = tile("fac%d" % u, [P, 2, width], F32)
            both = inv[u][:].unsqueeze(1).to_broadcast([P, 2, width])
            nc.vector.scalar_tensor_tensor(fac[u][:], den[u][:], 4.0 * DOWN, both, ALU.mult, ALU.mult)

        def result(u, i):
            b, a = units[u]
            c0, c1 = BLOCKS[b]
            t = 2 * a + i
            nc.vector.tensor_tensor(res[b][:, t, :], ex[t][:, c0:c1], fac[u][:, 1 - i], ALU.mult)
            if i == 1:
                nc.sync.dma_start(out=out_rows[:, 2 * a : 2 * a + 2, c0:c1], in_=res[b][:, 2 * a : 2 * a + 2, :])

        def hand_on(b):
            c0, c1 = BLOCKS[b]
            rounded = tile("rounded%d" % b, [P, c1 - c0, PACK], BF16)
            if b < len(BLOCKS) - 1:
                nc.scalar.copy(out=rounded[:], in_=res[b][:].rearrange("p t j -> p j t"))
            else:
                nc.vector.tensor_copy(out=rounded[:], in_=res[b][:].rearrange("p t j -> p j t"))
            nc.vector.quantize_mx(
                out=ow[:, c0:c1].bitcast(FP8X4), scales=osc[:, c0:c1], in_=rounded[:].rearrange("p j t -> p (j t)")
            )

        for u in range(len(units)):
            fetch(u)
        for u in range(len(units) + 1):
            ahead, behind = u < len(units), u > 0
            if ahead:
                add_pairs(u)
            if behind:
                factors(u - 1)
            if ahead:
                denominators(u)
            if behind:
                result(u - 1, 0)
            if ahead:
                product(u)
            if behind:
                result(u - 1, 1)
            if ahead:
                invert(u)
        for b in range(len(BLOCKS)):
            hand_on(b)
        nc.scalar.dma_start(out=out_words, in_=ow[:].bitcast(I32))
        scale_rows = out_2[0].bitcast(I32)
        for q in range(4):
            queue = nc.sync if q % 2 == 0 else nc.scalar
            queue.dma_start(out=scale_rows[4 * q : 4 * q + 4, :], in_=osc[QUAD * q : QUAD * q + 4, :].bitcast(I32))
